import numpy as np
import ml_dtypes


def mxq(x, axis, fmt="e4m3"):
    dtype, down = {"e4m3": (ml_dtypes.float8_e4m3fn, 7), "e5m2": (ml_dtypes.float8_e5m2, 14)}[fmt]
    v = np.moveaxis(np.asarray(x, np.float32).astype(ml_dtypes.bfloat16).astype(np.float64), axis, -1)
    blocks = v.reshape(v.shape[:-1] + (-1, 32))
    amax = np.abs(blocks).max(-1, keepdims=True)
    byte = np.maximum(np.where(amax > 0, np.frexp(amax)[1] - 1 + 127, 0) - down, 1)
    scale = np.exp2(byte - 127.0)
    codes = (blocks / scale).astype(np.float32).astype(dtype).astype(np.float64)
    return np.moveaxis((codes * scale).reshape(v.shape), -1, axis)


WIDE = False


def mx_kscale(k):
    if not WIDE:
        return np.ones(k)
    levels = np.array([10, -10, 5, -5, 0])
    if k % 512:
        return np.exp2(np.random.permutation(np.resize(levels, k // 32))).repeat(32)
    a = np.empty((k // 512, 16))
    for p in range(k // 512):
        a[p, :8] = np.random.permutation(np.resize(levels, 8))
        for g in range(8):
            far = levels[np.abs(levels - a[p, g]) >= 10]
            a[p, g + 8] = far[np.random.randint(len(far))]
    return np.exp2(a.ravel()).repeat(32)


def f64(x):
    return np.asarray(x).astype(np.float64)


def striped(idx):
    return np.tile(idx.reshape(-1, 16).T, (8, 1)).astype(np.uint16)


def unstriped(offs):
    return offs[:16].T.reshape(-1).astype(np.int64)


E2M1 = np.array([0.0, 0.5, 1.0, 1.5, 2.0, 3.0, 4.0, 6.0, -0.0, -0.5, -1.0, -1.5, -2.0, -3.0, -4.0, -6.0])


def pack_weight(w, fmt):
    k, n = w.shape
    w = f64(np.asarray(w, np.float32).astype(ml_dtypes.bfloat16)).reshape(k // 32, 32, n)
    amax = np.abs(w).max(1)
    if fmt == "e4m3":
        byte = np.frexp(amax)[1] - 1 + 127 - 7
    else:
        mant, ex = np.frexp(amax / 6.0)
        byte = np.where(mant > 0.5, ex, ex - 1) + 127
    byte = np.clip(np.where(amax > 0, byte, 1), 1, 254)
    scaled = (w * np.exp2(127.0 - byte)[:, None, :]).reshape(k, n).astype(np.float32)
    by_word = np.ascontiguousarray(scaled.reshape(k // 512, 128, 4, n).transpose(0, 1, 3, 2))
    if fmt == "e4m3":
        words = by_word.astype(ml_dtypes.float8_e4m3fn).view(np.uint8)
    else:
        c = by_word.astype(ml_dtypes.float4_e2m1fn).view(np.uint8) & 0xF
        words = (c[..., 0::2] | (c[..., 1::2] << 4)).reshape(k // 512, 128, 2 * n)
    return np.ascontiguousarray(words), np.ascontiguousarray(byte.astype(np.uint8).reshape(k // 512, 16, n))


def unpack_weight(words, scales, fmt):
    g, _, n = scales.shape
    words = np.ascontiguousarray(words).reshape(g, 128, n, -1)
    if fmt == "e4m3":
        vals = words.view(ml_dtypes.float8_e4m3fn).astype(np.float64)
    else:
        nib = np.empty((g, 128, n, 4), np.uint8)
        nib[..., 0::2] = words & 0xF
        nib[..., 1::2] = words >> 4
        vals = E2M1[nib]
    vals = vals * np.repeat(np.exp2(scales.astype(np.float64) - 127.0), 8, axis=1)[..., None]
    return vals.transpose(0, 1, 3, 2).reshape(g * 512, n)


def silu(v):
    return v / (1.0 + np.exp(-np.maximum(v, -700.0)))


K, T, E, C, H, N = 512, 768, 12, 256, 512, 128
TOP = 4


def by_expert(wq, xq):
    return np.concatenate([wq[e].T @ xq[:, e * C:(e + 1) * C] for e in range(E)], axis=1)


def setup_inputs():
    n = np.random.standard_normal
    s = mx_kscale(K)[:, None]
    u = mx_kscale(H)
    deal = np.repeat(np.arange(E), C).reshape(TOP, T)[:, np.random.permutation(T)]
    deal = np.take_along_axis(deal, np.argsort(np.random.rand(TOP, T), axis=0), axis=0)
    for _ in range(8):
        s_, t_ = np.random.permutation(T).reshape(2, -1); r = np.random.randint(TOP, size=T // 2); x, y = deal[r, s_].copy(), deal[r, t_].copy()
        ok = ~((deal[:, s_] == y).any(0) | (deal[:, t_] == x).any(0)); deal[r[ok], s_[ok]] = y[ok]; deal[r[ok], t_[ok]] = x[ok]
    order = np.lexsort((np.random.rand(TOP * T), deal.reshape(-1)))
    slot_token = order % T; pos = np.empty(TOP * T, np.int64); pos[order] = np.arange(TOP * T); pos = pos.reshape(TOP, T)
    g = np.random.uniform(0.5, 1.5, (TOP, T)); g = g / g.sum(0)
    w1 = [pack_weight(m, "e2m1") for m in n((E, K, H)) / np.sqrt(K) / s[None] * u[None, None, :]]
    w2 = [pack_weight(m, "e2m1") for m in n((E, H, N)) / np.sqrt(H) / u[None, :, None]]
    return {
        "xT": (n((K, T)) * s).astype(np.float32),
        "w1_words": np.stack([m[0] for m in w1]),
        "w1_scales": np.stack([m[1] for m in w1]),
        "w2_words": np.stack([m[0] for m in w2]),
        "w2_scales": np.stack([m[1] for m in w2]),
        "gate": np.stack([np.tile(r, (N, 1)) for r in g]).astype(np.float32),
        "offs": striped(slot_token),
        "pos1": striped(pos[0]),
        "pos2": striped(pos[1]),
        "pos3": striped(pos[2]),
        "pos4": striped(pos[3]),
    }


def reference(xT, w1_words, w1_scales, w2_words, w2_scales, gate, offs, pos1, pos2, pos3, pos4):
    idx = unstriped(offs)
    w1 = np.stack([unpack_weight(w1_words[e], w1_scales[e], "e2m1") for e in range(E)])
    w2 = np.stack([unpack_weight(w2_words[e], w2_scales[e], "e2m1") for e in range(E)])
    xq = mxq(f64(xT)[:, idx], 0, "e4m3")
    h = silu(by_expert(w1, xq))
    y = by_expert(w2, mxq(h, 0, "e4m3"))
    return sum(f64(gate[r]) * y[:, unstriped(p)] for r, p in enumerate((pos1, pos2, pos3, pos4)))

@@ -1,0 +1,244 @@
+from contextlib import ExitStack
+
+import concourse.mybir as mybir
+from concourse.masks import make_identity
+
+K, T, E, C, H, N = 512, 768, 12, 256, 512, 128
+TOP = 4
+P = 128
+S = E * C
+FLOPS = 2 * S * (K * H + H * N)
+
+F32 = mybir.dt.float32
+BF16 = mybir.dt.bfloat16
+U32 = mybir.dt.uint32
+I32 = mybir.dt.int32
+U16 = mybir.dt.uint16
+U8 = mybir.dt.uint8
+FP8X4 = mybir.dt.float8_e4m3fn_x4
+FP4X4 = mybir.dt.float4_e2m1fn_x4
+SILU = mybir.ActivationFunctionType.Silu
+MULT = mybir.AluOpType.mult
+ADD = mybir.AluOpType.add
+
+X_CHUNKS = [(0, 256), (256, 256), (512, 128), (640, 128)]
+X_CAST_ON_SCALAR = (0, 2)
+GATHERS = [(0, 128), (128, 128)] + [(a, 256) for a in range(256, S, 256)]
+W1_LOADS = [(0, 1), (1, 2), (2, 4), (4, 8), (8, 12)]
+W2_LOADS = [(0, 4), (4, 12)]
+TAIL = [(0, 384), (384, 384)]
+Y_ON_SCALAR = (1, 4, 7)
+
+
+def tile_moe_tk_mlp_silu_kernel(
+    tc, xT, w1_words, w1_scales, w2_words, w2_scales, gate, offs, pos1, pos2, pos3, pos4, out
+):
+    nc = tc.nc
+    with ExitStack() as ctx:
+        lists = ctx.enter_context(tc.tile_pool(name="lists", bufs=1))
+        keep = ctx.enter_context(tc.tile_pool(name="keep", bufs=1))
+        ring = ctx.enter_context(tc.tile_pool(name="ring", bufs=4))
+        g_ring = ctx.enter_context(tc.tile_pool(name="g_ring", bufs=3))
+        a_psum = ctx.enter_context(tc.psum_pool(name="a_psum", bufs=4))
+        t_psum = ctx.enter_context(tc.psum_pool(name="t_psum", bufs=2))
+        y_psum = ctx.enter_context(tc.psum_pool(name="y_psum", bufs=2))
+
+        offs_t = lists.tile([P, S // 16], U16, name="offs_t")
+        nc.sync.dma_start(offs_t[:], offs)
+
+        warm = keep.tile([P, 1], F32, name="warm")
+        warm_out = keep.tile([P, 1], F32, name="warm_out")
+        nc.vector.memset(warm[:], 0.0)
+        nc.scalar.activation(out=warm_out[:], in_=warm[:], func=SILU)
+
+        w1_s = keep.tile([P, E, H], U8, name="w1_s", align_bytes=64)
+        w2_s = keep.tile([P, E, N], U8, name="w2_s", align_bytes=64)
+        nc.vector.memset(w1_s[:].bitcast(I32), 0)
+        nc.vector.memset(w2_s[:].bitcast(I32), 0)
+        x_scales = keep.tile([P, T], U8, name="x_scales", align_bytes=64)
+        nc.gpsimd.memset(x_scales[:], 0)
+        ident = keep.tile([P, P], F32, name="ident")
+        make_identity(nc, ident[:])
+
+        x_view = xT.rearrange("(p j) t -> p j t", j=4)
+        x_raw = []
+        for i, (a, n) in enumerate(X_CHUNKS):
+            raw = keep.tile([P, 4, n], F32, name=f"x_raw{i}")
+            nc.sync.dma_start(raw[:], x_view[:, :, a : a + n])
+            x_raw.append(raw)
+        for q in range(4):
+            rows = w1_scales[:, 0, 4 * q : 4 * q + 4, :].rearrange("e q i -> q e i")
+            nc.sync.dma_start(w1_s[32 * q : 32 * q + 4, :, :].bitcast(I32), rows.bitcast(I32))
+        w1 = []
+        for a, b in W1_LOADS[:2]:
+            words = keep.tile([P, b - a, 2 * H], U8, name=f"w1_{a}", align_bytes=64)
+            nc.sync.dma_start(words[:], w1_words[a:b, 0].rearrange("e p c -> p e c"))
+            w1.extend([words[:, e - a, :] for e in range(a, b)])
+        for q in range(4):
+            rows = w2_scales[:, 0, 4 * q : 4 * q + 4, :].rearrange("e q n -> q e n")
+            nc.sync.dma_start(w2_s[32 * q : 32 * q + 4, :, :].bitcast(I32), rows.bitcast(I32))
+        w2 = []
+        for k in range(3):
+            if k < 2:
+                a, b = W2_LOADS[k]
+                words = keep.tile([P, b - a, 2 * N], U8, name=f"w2_{a}", align_bytes=64)
+                nc.sync.dma_start(words[:], w2_words[a:b, 0].rearrange("e p c -> p e c"))
+                w2.extend([words[:, e - a, :] for e in range(a, b)])
+            a, b = W1_LOADS[2 + k]
+            words = keep.tile([P, b - a, 2 * H], U8, name=f"w1_{a}", align_bytes=64)
+            nc.sync.dma_start(words[:], w1_words[a:b, 0].rearrange("e p c -> p e c"))
+            w1.extend([words[:, e - a, :] for e in range(a, b)])
+        pos_t = []
+        for r, pos in enumerate((pos1, pos2, pos3, pos4)):
+            lst = lists.tile([P, T // 16], U16, name=f"pos_t{r}")
+            nc.sync.dma_start(lst[:], pos)
+            pos_t.append(lst)
+        gates = []
+        for r in range(TOP):
+            g_t = keep.tile([P, T], F32, name=f"gate_t{r}")
+            nc.sync.dma_start(g_t[:], gate[r])
+            gates.append(g_t)
+
+        x_words = keep.tile([P, T], U32, name="x_words", align_bytes=64)
+        x_bf = []
+        for i, (a, n) in enumerate(X_CHUNKS):
+            xb = keep.tile([P, n, 4], BF16, name=f"x_bf{i}", align_bytes=64)
+            x_bf.append(xb)
+
+        def cast(i):
+            src = x_raw[i][:].rearrange("p j t -> p t j")
+            if i in X_CAST_ON_SCALAR:
+                nc.scalar.copy(out=x_bf[i][:], in_=src)
+            else:
+                nc.vector.tensor_copy(out=x_bf[i][:], in_=src)
+
+        def quantise_x(i):
+            a, n = X_CHUNKS[i]
+            nc.vector.quantize_mx(
+                out=x_words[:, a : a + n].bitcast(FP8X4),
+                scales=x_scales[:, a : a + n],
+                in_=x_bf[i][:].rearrange("p t j -> p (t j)"),
+            )
+
+        cast(0)
+        cast(1)
+        quantise_x(0)
+        quantise_x(1)
+        cast(2)
+        cast(3)
+        quantise_x(2)
+        quantise_x(3)
+
+        g_words, g_scales = {}, {}
+
+        def gather(i):
+            a, n = GATHERS[i]
+            words = g_ring.tile([P, n], U32, name=f"g_words_{n}", align_bytes=64)
+            nc.vector.tensor_copy(words[:], x_words[:].indirect(offs_t[:, a // 16 : (a + n) // 16]))
+            scales = g_ring.tile([P, n], U8, name=f"g_scales_{n}", align_bytes=64)
+            nc.vector.tensor_copy(scales[:], x_scales[:].indirect(offs_t[:, a // 16 : (a + n) // 16]))
+            for s in range(0, n, P):
+                g_words[(a + s) // P] = words[:, s : s + P]
+                g_scales[(a + s) // P] = scales[:, s : s + P]
+
+        y_all = keep.tile([P, S], F32, name="y_all")
+        h_bf, turned, h_in, h_words, h_scales, y_ps = {}, {}, {}, {}, {}, {}
+
+        def first(e):
+            for g in (2 * e, 2 * e + 1):
+                acc = a_psum.tile([P, H], F32, name="acc")
+                nc.tensor.matmul_mx(
+                    out=acc[:],
+                    lhsT=g_words[g].bitcast(FP8X4),
+                    lhsT_scale=g_scales[g],
+                    rhs=w1[e].bitcast(FP4X4),
+                    rhs_scale=w1_s[:, e, :],
+                    start=True,
+                    stop=True,
+                )
+                h = ring.tile([P, H], BF16, name="h", align_bytes=64)
+                nc.scalar.activation(
+                    out=h[:].rearrange("s (u p e) -> s u p e", u=2, e=2),
+                    in_=acc[:].rearrange("s (p u e) -> s u p e", u=2, e=2),
+                    func=SILU,
+                )
+                h_bf[g] = h
+
+        def turn(e):
+            bank = t_psum.tile([P, 2, 2, P], F32, name="bank")
+            for g in range(2):
+                words = h_bf[2 * e + g][:].bitcast(F32)
+                for u in range(2):
+                    nc.tensor.transpose(bank[:, g, u, :], words[:, u * P : (u + 1) * P], ident[:])
+            hin = ring.tile([P, C, 4], BF16, name="hin", align_bytes=64)
+            nc.scalar.copy(
+                out=hin[:].bitcast(F32).rearrange("p (g r) u -> p g r u", g=2),
+                in_=bank[:].rearrange("p g u r -> p g r u"),
+            )
+            h_in[e] = hin
+
+        def quantise(e):
+            hw = ring.tile([P, C], U32, name="hw", align_bytes=64)
+            hs = ring.tile([P, C], U8, name="hs", align_bytes=64)
+            nc.vector.quantize_mx(
+                out=hw[:].bitcast(FP8X4), scales=hs[:], in_=h_in[e][:].rearrange("p s j -> p (s j)")
+            )
+            h_words[e], h_scales[e] = hw, hs
+
+        def second(e):
+            yp = y_psum.tile([P, C], F32, name="yp")
+            nc.tensor.matmul_mx(
+                out=yp[:],
+                lhsT=w2[e].bitcast(FP4X4),
+                lhsT_scale=w2_s[:, e, :],
+                rhs=h_words[e][:].bitcast(FP8X4),
+                rhs_scale=h_scales[e][:],
+                start=True,
+                stop=True,
+            )
+            y_ps[e] = yp
+
+        def keep_y(e):
+            dst = y_all[:, e * C : (e + 1) * C]
+            if e in Y_ON_SCALAR:
+                nc.scalar.copy(out=dst, in_=y_ps[e][:])
+            else:
+                nc.vector.tensor_copy(out=dst, in_=y_ps[e][:])
+
+        done = 0
+        for step in range(E + 3):
+            while done < len(GATHERS) and GATHERS[done][0] <= (step + 1) * C:
+                gather(done)
+                done += 1
+            if step < E:
+                first(step)
+            if 1 <= step <= E:
+                turn(step - 1)
+            if 2 <= step <= E + 1:
+                quantise(step - 2)
+                second(step - 2)
+            if 3 <= step:
+                keep_y(step - 3)
+
+        prod = []
+        part = keep.tile([P, T], F32, name="part")
+        total = keep.tile([P, T], F32, name="total")
+        res = keep.tile([P, T], F32, name="res")
+
+        def weigh(r):
+            term = keep.tile([P, T], F32, name=f"term{r}")
+            nc.vector.tensor_tensor(term[:], y_all[:].indirect(pos_t[r][:]), gates[r][:], MULT)
+            prod.append(term)
+
+        weigh(0)
+        weigh(1)
+        weigh(2)
+        nc.vector.tensor_tensor(part[:], prod[0][:], prod[1][:], ADD)
+        weigh(3)
+        for a, n in TAIL:
+            cols = slice(a, a + n)
+            nc.vector.tensor_tensor(total[:, cols], part[:, cols], prod[2][:, cols], ADD)
+        for a, n in TAIL:
+            cols = slice(a, a + n)
+            nc.vector.tensor_tensor(res[:, cols], total[:, cols], prod[3][:, cols], ADD)
+            nc.sync.dma_start(out[:, cols], res[:, cols])

@@ -26,8 +26,11 @@ X_CAST_ON_SCALAR = (0, 2)
 GATHERS = [(0, 128), (128, 128)] + [(a, 256) for a in range(256, S, 256)]
 W1_LOADS = [(0, 1), (1, 2), (2, 4), (4, 8), (8, 12)]
 W2_LOADS = [(0, 4), (4, 12)]
+UNITS = [(2 * e, 2) for e in range(11)] + [(22, 1), (23, 1)]
+Y_BANKS = [(u,) for u in range(13)]
+TURN_ON_VECTOR = (11, 12)
+Y_ON_SCALAR = (2, 5, 8)
 TAIL = [(0, 384), (384, 384)]
-Y_ON_SCALAR = (1, 4, 7)
 
 
 def tile_moe_tk_mlp_silu_kernel(
@@ -42,9 +45,6 @@ def tile_moe_tk_mlp_silu_kernel(
         a_psum = ctx.enter_context(tc.psum_pool(name="a_psum", bufs=4))
         t_psum = ctx.enter_context(tc.psum_pool(name="t_psum", bufs=2))
         y_psum = ctx.enter_context(tc.psum_pool(name="y_psum", bufs=2))
-
-        offs_t = lists.tile([P, S // 16], U16, name="offs_t")
-        nc.sync.dma_start(offs_t[:], offs)
 
         warm = keep.tile([P, 1], F32, name="warm")
         warm_out = keep.tile([P, 1], F32, name="warm_out")
@@ -66,28 +66,37 @@ def tile_moe_tk_mlp_silu_kernel(
             raw = keep.tile([P, 4, n], F32, name=f"x_raw{i}")
             nc.sync.dma_start(raw[:], x_view[:, :, a : a + n])
             x_raw.append(raw)
-        for q in range(4):
-            rows = w1_scales[:, 0, 4 * q : 4 * q + 4, :].rearrange("e q i -> q e i")
-            nc.sync.dma_start(w1_s[32 * q : 32 * q + 4, :, :].bitcast(I32), rows.bitcast(I32))
-        w1 = []
-        for a, b in W1_LOADS[:2]:
+        offs_t = lists.tile([P, S // 16], U16, name="offs_t")
+        nc.sync.dma_start(offs_t[:], offs)
+        w1, w2 = [], []
+
+        def load_w1_scales(a, b):
+            for q in range(4):
+                rows = w1_scales[a:b, 0, 4 * q : 4 * q + 4, :].rearrange("e q i -> q e i")
+                nc.sync.dma_start(w1_s[32 * q : 32 * q + 4, a:b, :].bitcast(I32), rows.bitcast(I32))
+
+        def load_w1(a, b):
             words = keep.tile([P, b - a, 2 * H], U8, name=f"w1_{a}", align_bytes=64)
             nc.sync.dma_start(words[:], w1_words[a:b, 0].rearrange("e p c -> p e c"))
             w1.extend([words[:, e - a, :] for e in range(a, b)])
+
+        def load_w2(a, b):
+            words = keep.tile([P, b - a, 2 * N], U8, name=f"w2_{a}", align_bytes=64)
+            nc.sync.dma_start(words[:], w2_words[a:b, 0].rearrange("e p c -> p e c"))
+            w2.extend([words[:, e - a, :] for e in range(a, b)])
+
+        load_w1_scales(0, 3)
+        load_w1(0, 1)
+        load_w1(1, 2)
+        load_w1_scales(3, 12)
         for q in range(4):
             rows = w2_scales[:, 0, 4 * q : 4 * q + 4, :].rearrange("e q n -> q e n")
             nc.sync.dma_start(w2_s[32 * q : 32 * q + 4, :, :].bitcast(I32), rows.bitcast(I32))
-        w2 = []
-        for k in range(3):
-            if k < 2:
-                a, b = W2_LOADS[k]
-                words = keep.tile([P, b - a, 2 * N], U8, name=f"w2_{a}", align_bytes=64)
-                nc.sync.dma_start(words[:], w2_words[a:b, 0].rearrange("e p c -> p e c"))
-                w2.extend([words[:, e - a, :] for e in range(a, b)])
-            a, b = W1_LOADS[2 + k]
-            words = keep.tile([P, b - a, 2 * H], U8, name=f"w1_{a}", align_bytes=64)
-            nc.sync.dma_start(words[:], w1_words[a:b, 0].rearrange("e p c -> p e c"))
-            w1.extend([words[:, e - a, :] for e in range(a, b)])
+        load_w2(0, 4)
+        load_w1(2, 4)
+        load_w1(4, 8)
+        load_w2(4, 12)
+        load_w1(8, 12)
         pos_t = []
         for r, pos in enumerate((pos1, pos2, pos3, pos4)):
             lst = lists.tile([P, T // 16], U16, name=f"pos_t{r}")
@@ -142,10 +151,12 @@ def tile_moe_tk_mlp_silu_kernel(
                 g_scales[(a + s) // P] = scales[:, s : s + P]
 
         y_all = keep.tile([P, S], F32, name="y_all")
-        h_bf, turned, h_in, h_words, h_scales, y_ps = {}, {}, {}, {}, {}, {}
+        h_bf, h_in, h_words, h_scales, y_ps = {}, {}, {}, {}, {}
 
-        def first(e):
-            for g in (2 * e, 2 * e + 1):
+        def first(unit):
+            g0, count = UNITS[unit]
+            for g in range(g0, g0 + count):
+                e = g // 2
                 acc = a_psum.tile([P, H], F32, name="acc")
                 nc.tensor.matmul_mx(
                     out=acc[:],
@@ -164,57 +175,70 @@ def tile_moe_tk_mlp_silu_kernel(
                 )
                 h_bf[g] = h
 
-        def turn(e):
+        def turn(unit):
+            g0, count = UNITS[unit]
             bank = t_psum.tile([P, 2, 2, P], F32, name="bank")
-            for g in range(2):
-                words = h_bf[2 * e + g][:].bitcast(F32)
+            for g in range(count):
+                words = h_bf[g0 + g][:].bitcast(F32)
                 for u in range(2):
                     nc.tensor.transpose(bank[:, g, u, :], words[:, u * P : (u + 1) * P], ident[:])
-            hin = ring.tile([P, C, 4], BF16, name="hin", align_bytes=64)
-            nc.scalar.copy(
-                out=hin[:].bitcast(F32).rearrange("p (g r) u -> p g r u", g=2),
-                in_=bank[:].rearrange("p g u r -> p g r u"),
-            )
-            h_in[e] = hin
+            hin = ring.tile([P, count * P, 4], BF16, name=f"hin{count}", align_bytes=64)
+            dst = hin[:].bitcast(F32).rearrange("p (g r) u -> p g r u", g=count)
+            src = bank[:, 0:count].rearrange("p g u r -> p g r u")
+            if unit in TURN_ON_VECTOR:
+                nc.vector.tensor_copy(out=dst, in_=src)
+            else:
+                nc.scalar.copy(out=dst, in_=src)
+            h_in[unit] = hin
 
-        def quantise(e):
-            hw = ring.tile([P, C], U32, name="hw", align_bytes=64)
-            hs = ring.tile([P, C], U8, name="hs", align_bytes=64)
+        def quantise(unit):
+            n = UNITS[unit][1] * P
+            hw = ring.tile([P, n], U32, name=f"hw{n}", align_bytes=64)
+            hs = ring.tile([P, n], U8, name=f"hs{n}", align_bytes=64)
             nc.vector.quantize_mx(
-                out=hw[:].bitcast(FP8X4), scales=hs[:], in_=h_in[e][:].rearrange("p s j -> p (s j)")
+                out=hw[:].bitcast(FP8X4), scales=hs[:], in_=h_in[unit][:].rearrange("p s j -> p (s j)")
             )
-            h_words[e], h_scales[e] = hw, hs
+            h_words[unit], h_scales[unit] = hw, hs
 
-        def second(e):
-            yp = y_psum.tile([P, C], F32, name="yp")
+        def second(unit):
+            g0, count = UNITS[unit]
+            e = g0 // 2
+            bank = [b for b in Y_BANKS if unit in b][0]
+            if unit == bank[0]:
+                y_ps[bank] = y_psum.tile([P, 512], F32, name="yp")
+            at = (g0 - UNITS[bank[0]][0]) * P
             nc.tensor.matmul_mx(
-                out=yp[:],
+                out=y_ps[bank][:, at : at + count * P],
                 lhsT=w2[e].bitcast(FP4X4),
                 lhsT_scale=w2_s[:, e, :],
-                rhs=h_words[e][:].bitcast(FP8X4),
-                rhs_scale=h_scales[e][:],
+                rhs=h_words[unit][:].bitcast(FP8X4),
+                rhs_scale=h_scales[unit][:],
                 start=True,
                 stop=True,
             )
-            y_ps[e] = yp
 
-        def keep_y(e):
-            dst = y_all[:, e * C : (e + 1) * C]
-            if e in Y_ON_SCALAR:
-                nc.scalar.copy(out=dst, in_=y_ps[e][:])
-            else:
-                nc.vector.tensor_copy(out=dst, in_=y_ps[e][:])
+        def keep_y(unit):
+            bank = [b for b in Y_BANKS if unit in b][0]
+            if unit == bank[-1]:
+                a = UNITS[bank[0]][0] * P
+                n = sum([UNITS[u][1] for u in bank]) * P
+                if unit in Y_ON_SCALAR:
+                    nc.scalar.copy(out=y_all[:, a : a + n], in_=y_ps[bank][:, 0:n])
+                else:
+                    nc.vector.tensor_copy(out=y_all[:, a : a + n], in_=y_ps[bank][:, 0:n])
 
         done = 0
-        for step in range(E + 3):
-            while done < len(GATHERS) and GATHERS[done][0] <= (step + 1) * C:
+        steps = len(UNITS)
+        for step in range(steps + 3):
+            ahead = UNITS[min(step + 1, steps - 1)][0] * P
+            while done < len(GATHERS) and GATHERS[done][0] <= ahead:
                 gather(done)
                 done += 1
-            if step < E:
+            if step < steps:
                 first(step)
-            if 1 <= step <= E:
+            if 1 <= step <= steps:
                 turn(step - 1)
-            if 2 <= step <= E + 1:
+            if 2 <= step <= steps + 1:
                 quantise(step - 2)
                 second(step - 2)
             if 3 <= step:

@@ -24,12 +24,27 @@ ADD = mybir.AluOpType.add
 X_CHUNKS = [(0, 256), (256, 256), (512, 128), (640, 128)]
 X_CAST_ON_SCALAR = (0, 2)
 GATHERS = [(0, 128), (128, 128)] + [(a, 256) for a in range(256, S, 256)]
-W1_LOADS = [(0, 1), (1, 2), (2, 4), (4, 8), (8, 12)]
-W2_LOADS = [(0, 4), (4, 12)]
 UNITS = [(2 * e, 2) for e in range(11)] + [(22, 1), (23, 1)]
 Y_BANKS = [(u,) for u in range(13)]
-TURN_ON_VECTOR = (11, 12)
-Y_ON_SCALAR = (2, 5, 8)
+Y_ON_VECTOR = (12,)
+TURNED = (0, 1, 4, 8)
+LOADS = [
+    ("w1", 2, 4),
+    ("x", 0, 0),
+    ("x", 1, 0),
+    ("s1", 0, 4),
+    ("x", 2, 0),
+    ("x", 3, 0),
+    ("offs", 0, 0),
+    ("w1", 0, 2),
+    ("s1", 4, 12),
+    ("s2", 0, 12),
+    ("w2", 0, 4),
+    ("w1", 4, 8),
+    ("w1", 8, 12),
+    ("w2", 4, 12),
+]
+PERMS = [(2, 4), (5, 8), (9, 12)]
 TAIL = [(0, 384), (384, 384)]
 
 
@@ -42,8 +57,8 @@ def tile_moe_tk_mlp_silu_kernel(
         keep = ctx.enter_context(tc.tile_pool(name="keep", bufs=1))
         ring = ctx.enter_context(tc.tile_pool(name="ring", bufs=4))
         g_ring = ctx.enter_context(tc.tile_pool(name="g_ring", bufs=3))
-        a_psum = ctx.enter_context(tc.psum_pool(name="a_psum", bufs=4))
-        t_psum = ctx.enter_context(tc.psum_pool(name="t_psum", bufs=2))
+        a_psum = ctx.enter_context(tc.psum_pool(name="a_psum", bufs=5))
+        t_psum = ctx.enter_context(tc.psum_pool(name="t_psum", bufs=1))
         y_psum = ctx.enter_context(tc.psum_pool(name="y_psum", bufs=2))
 
         warm = keep.tile([P, 1], F32, name="warm")
@@ -51,52 +66,51 @@ def tile_moe_tk_mlp_silu_kernel(
         nc.vector.memset(warm[:], 0.0)
         nc.scalar.activation(out=warm_out[:], in_=warm[:], func=SILU)
 
+        raw_s = keep.tile([P, E, H], U8, name="raw_s", align_bytes=64)
         w1_s = keep.tile([P, E, H], U8, name="w1_s", align_bytes=64)
         w2_s = keep.tile([P, E, N], U8, name="w2_s", align_bytes=64)
-        nc.vector.memset(w1_s[:].bitcast(I32), 0)
+        for a in range(0, E, 4):
+            nc.vector.memset(raw_s[:, a : a + 4, :].bitcast(I32), 0)
         nc.vector.memset(w2_s[:].bitcast(I32), 0)
         x_scales = keep.tile([P, T], U8, name="x_scales", align_bytes=64)
         nc.gpsimd.memset(x_scales[:], 0)
         ident = keep.tile([P, P], F32, name="ident")
         make_identity(nc, ident[:])
 
-        x_view = xT.rearrange("(p j) t -> p j t", j=4)
-        x_raw = []
-        for i, (a, n) in enumerate(X_CHUNKS):
-            raw = keep.tile([P, 4, n], F32, name=f"x_raw{i}")
-            nc.sync.dma_start(raw[:], x_view[:, :, a : a + n])
-            x_raw.append(raw)
         offs_t = lists.tile([P, S // 16], U16, name="offs_t")
-        nc.sync.dma_start(offs_t[:], offs)
-        w1, w2 = [], []
+        x_view = xT.rearrange("(p j) t -> p j t", j=4)
+        x_raw = {}
+        raw_w, w2 = {}, {}
 
-        def load_w1_scales(a, b):
-            for q in range(4):
-                rows = w1_scales[a:b, 0, 4 * q : 4 * q + 4, :].rearrange("e q i -> q e i")
-                nc.sync.dma_start(w1_s[32 * q : 32 * q + 4, a:b, :].bitcast(I32), rows.bitcast(I32))
+        def load(kind, a, b):
+            if kind == "offs":
+                nc.sync.dma_start(offs_t[:], offs)
+            elif kind == "x":
+                raw = keep.tile([P, 4, X_CHUNKS[a][1]], F32, name=f"x_raw{a}")
+                c = X_CHUNKS[a][0]
+                nc.sync.dma_start(raw[:], x_view[:, :, c : c + X_CHUNKS[a][1]])
+                x_raw[a] = raw
+            elif kind == "s1":
+                for q in range(4):
+                    rows = w1_scales[a:b, 0, 4 * q : 4 * q + 4, :].rearrange("e q i -> q e i")
+                    nc.sync.dma_start(raw_s[32 * q : 32 * q + 4, a:b, :].bitcast(I32), rows.bitcast(I32))
+            elif kind == "s2":
+                for q in range(4):
+                    rows = w2_scales[a:b, 0, 4 * q : 4 * q + 4, :].rearrange("e q n -> q e n")
+                    nc.sync.dma_start(w2_s[32 * q : 32 * q + 4, a:b, :].bitcast(I32), rows.bitcast(I32))
+            elif kind == "w1":
+                words = keep.tile([P, b - a, 2 * H], U8, name=f"raw_w{a}", align_bytes=64)
+                nc.sync.dma_start(words[:], w1_words[a:b, 0].rearrange("e p c -> p e c"))
+                for e in range(a, b):
+                    raw_w[e] = (words, e - a)
+            else:
+                words = keep.tile([P, b - a, 2 * N], U8, name=f"w2_{a}", align_bytes=64)
+                nc.sync.dma_start(words[:], w2_words[a:b, 0].rearrange("e p c -> p e c"))
+                for e in range(a, b):
+                    w2[e] = words[:, e - a, :]
 
-        def load_w1(a, b):
-            words = keep.tile([P, b - a, 2 * H], U8, name=f"w1_{a}", align_bytes=64)
-            nc.sync.dma_start(words[:], w1_words[a:b, 0].rearrange("e p c -> p e c"))
-            w1.extend([words[:, e - a, :] for e in range(a, b)])
-
-        def load_w2(a, b):
-            words = keep.tile([P, b - a, 2 * N], U8, name=f"w2_{a}", align_bytes=64)
-            nc.sync.dma_start(words[:], w2_words[a:b, 0].rearrange("e p c -> p e c"))
-            w2.extend([words[:, e - a, :] for e in range(a, b)])
-
-        load_w1_scales(0, 3)
-        load_w1(0, 1)
-        load_w1(1, 2)
-        load_w1_scales(3, 12)
-        for q in range(4):
-            rows = w2_scales[:, 0, 4 * q : 4 * q + 4, :].rearrange("e q n -> q e n")
-            nc.sync.dma_start(w2_s[32 * q : 32 * q + 4, :, :].bitcast(I32), rows.bitcast(I32))
-        load_w2(0, 4)
-        load_w1(2, 4)
-        load_w1(4, 8)
-        load_w2(4, 12)
-        load_w1(8, 12)
+        for kind, a, b in LOADS:
+            load(kind, a, b)
         pos_t = []
         for r, pos in enumerate((pos1, pos2, pos3, pos4)):
             lst = lists.tile([P, T // 16], U16, name=f"pos_t{r}")
@@ -107,6 +121,23 @@ def tile_moe_tk_mlp_silu_kernel(
             g_t = keep.tile([P, T], F32, name=f"gate_t{r}")
             nc.sync.dma_start(g_t[:], gate[r])
             gates.append(g_t)
+
+        w1 = {}
+
+        def permute(a, b):
+            words, at = raw_w[a]
+            n = b - a
+            turned = keep.tile([P, n, 2 * H], U8, name=f"w1_{a}", align_bytes=64)
+            nc.vector.tensor_copy(
+                out=turned[:].bitcast(U16).rearrange("p e (t m) -> p t e m", t=4),
+                in_=words[:, at : at + n, :].bitcast(U16).rearrange("p e (m t) -> p t e m", t=4),
+            )
+            nc.vector.tensor_copy(
+                out=w1_s[:, a:b, :].rearrange("p e (t m) -> p t e m", t=4),
+                in_=raw_s[:, a:b, :].rearrange("p e (m t) -> p t e m", t=4),
+            )
+            for e in range(a, b):
+                w1[e] = turned[:, e - a, :]
 
         x_words = keep.tile([P, T], U32, name="x_words", align_bytes=64)
         x_bf = []
@@ -155,25 +186,47 @@ def tile_moe_tk_mlp_silu_kernel(
 
         def first(unit):
             g0, count = UNITS[unit]
-            for g in range(g0, g0 + count):
-                e = g // 2
-                acc = a_psum.tile([P, H], F32, name="acc")
-                nc.tensor.matmul_mx(
-                    out=acc[:],
-                    lhsT=g_words[g].bitcast(FP8X4),
-                    lhsT_scale=g_scales[g],
-                    rhs=w1[e].bitcast(FP4X4),
-                    rhs_scale=w1_s[:, e, :],
-                    start=True,
-                    stop=True,
-                )
-                h = ring.tile([P, H], BF16, name="h", align_bytes=64)
+            e = g0 // 2
+            if e in TURNED:
+                words, at = raw_w[e]
+                for g in range(g0, g0 + count):
+                    acc = a_psum.tile([P, H], F32, name="acc")
+                    nc.tensor.matmul_mx(
+                        out=acc[:],
+                        lhsT=g_words[g].bitcast(FP8X4),
+                        lhsT_scale=g_scales[g],
+                        rhs=words[:, at, :].bitcast(FP4X4),
+                        rhs_scale=raw_s[:, e, :],
+                        start=True,
+                        stop=True,
+                    )
+                    h = ring.tile([P, H], BF16, name="h", align_bytes=64)
+                    nc.scalar.activation(
+                        out=h[:].rearrange("s (u p e) -> s u p e", u=2, e=2),
+                        in_=acc[:].rearrange("s (p u e) -> s u p e", u=2, e=2),
+                        func=SILU,
+                    )
+                    h_bf[g] = h
+                return
+            hin = ring.tile([P, count * P, 4], BF16, name=f"hin{count}", align_bytes=64)
+            for g in range(count):
+                acc = a_psum.tile([P, 4, P], F32, name="acc")
+                for t in range(4):
+                    nc.tensor.matmul_mx(
+                        out=acc[:, t, :],
+                        lhsT=w1[e][:, 2 * P * t : 2 * P * (t + 1)].bitcast(FP4X4),
+                        lhsT_scale=w1_s[:, e, P * t : P * (t + 1)],
+                        rhs=g_words[g0 + g].bitcast(FP8X4),
+                        rhs_scale=g_scales[g0 + g],
+                        start=True,
+                        stop=True,
+                    )
                 nc.scalar.activation(
-                    out=h[:].rearrange("s (u p e) -> s u p e", u=2, e=2),
-                    in_=acc[:].rearrange("s (p u e) -> s u p e", u=2, e=2),
+                    out=hin[:, g * P : (g + 1) * P, :],
+                    in_=acc[:].rearrange("p t s -> p s t"),
                     func=SILU,
                 )
-                h_bf[g] = h
+            h_in[unit] = hin
 
         def turn(unit):
             g0, count = UNITS[unit]
@@ -183,12 +236,10 @@ def tile_moe_tk_mlp_silu_kernel(
                 for u in range(2):
                     nc.tensor.transpose(bank[:, g, u, :], words[:, u * P : (u + 1) * P], ident[:])
             hin = ring.tile([P, count * P, 4], BF16, name=f"hin{count}", align_bytes=64)
-            dst = hin[:].bitcast(F32).rearrange("p (g r) u -> p g r u", g=count)
-            src = bank[:, 0:count].rearrange("p g u r -> p g r u")
-            if unit in TURN_ON_VECTOR:
-                nc.vector.tensor_copy(out=dst, in_=src)
-            else:
-                nc.scalar.copy(out=dst, in_=src)
+            nc.scalar.copy(
+                out=hin[:].bitcast(F32).rearrange("p (g r) u -> p g r u", g=count),
+                in_=bank[:, 0:count].rearrange("p g u r -> p g r u"),
+            )
             h_in[unit] = hin
 
         def quantise(unit):
@@ -222,21 +273,25 @@ def tile_moe_tk_mlp_silu_kernel(
             if unit == bank[-1]:
                 a = UNITS[bank[0]][0] * P
                 n = sum([UNITS[u][1] for u in bank]) * P
-                if unit in Y_ON_SCALAR:
-                    nc.scalar.copy(out=y_all[:, a : a + n], in_=y_ps[bank][:, 0:n])
-                else:
+                if unit in Y_ON_VECTOR:
                     nc.vector.tensor_copy(out=y_all[:, a : a + n], in_=y_ps[bank][:, 0:n])
+                else:
+                    nc.scalar.copy(out=y_all[:, a : a + n], in_=y_ps[bank][:, 0:n])
 
         done = 0
+        permuted = 0
         steps = len(UNITS)
         for step in range(steps + 3):
             ahead = UNITS[min(step + 1, steps - 1)][0] * P
             while done < len(GATHERS) and GATHERS[done][0] <= ahead:
                 gather(done)
                 done += 1
+            while permuted < len(PERMS) and PERMS[permuted][0] <= step + 2:
+                permute(*PERMS[permuted])
+                permuted += 1
             if step < steps:
                 first(step)
-            if 1 <= step <= steps:
+            if 1 <= step <= steps and UNITS[step - 1][0] // 2 in TURNED:
                 turn(step - 1)
             if 2 <= step <= steps + 1:
                 quantise(step - 2)

@@ -26,7 +26,7 @@ X_CAST_ON_SCALAR = (0, 2)
 GATHERS = [(0, 128), (128, 128)] + [(a, 256) for a in range(256, S, 256)]
 UNITS = [(2 * e, 2) for e in range(11)] + [(22, 1), (23, 1)]
 Y_BANKS = [(u,) for u in range(13)]
-Y_ON_VECTOR = (12,)
+Y_ON_VECTOR = (9, 10, 11, 12)
 TURNED = (0, 1, 4, 8)
 LOADS = [
     ("w1", 2, 4),
@@ -45,7 +45,7 @@ LOADS = [
     ("w2", 4, 12),
 ]
 PERMS = [(2, 4), (5, 8), (9, 12)]
-TAIL = [(0, 384), (384, 384)]
+TAIL = [(0, 512), (512, 256)]
 
 
 def tile_moe_tk_mlp_silu_kernel(

from contextlib import ExitStack

import concourse.mybir as mybir
from concourse.masks import make_identity

K, T, E, C, H, N = 512, 768, 12, 256, 512, 128
TOP = 4
P = 128
S = E * C
FLOPS = 2 * S * (K * H + H * N)

F32 = mybir.dt.float32
BF16 = mybir.dt.bfloat16
U32 = mybir.dt.uint32
I32 = mybir.dt.int32
U16 = mybir.dt.uint16
U8 = mybir.dt.uint8
FP8X4 = mybir.dt.float8_e4m3fn_x4
FP4X4 = mybir.dt.float4_e2m1fn_x4
SILU = mybir.ActivationFunctionType.Silu
MULT = mybir.AluOpType.mult
ADD = mybir.AluOpType.add

X_CHUNKS = [(0, 256), (256, 256), (512, 128), (640, 128)]
X_CAST_ON_SCALAR = (0, 2)
GATHERS = [(0, 128), (128, 128)] + [(a, 256) for a in range(256, S, 256)]
UNITS = [(2 * e, 2) for e in range(11)] + [(22, 1), (23, 1)]
Y_BANKS = [(u,) for u in range(13)]
Y_ON_VECTOR = (9, 10, 11, 12)
TURNED = (0, 1, 4, 8)
LOADS = [
    ("w1", 2, 4),
    ("x", 0, 0),
    ("x", 1, 0),
    ("s1", 0, 4),
    ("x", 2, 0),
    ("x", 3, 0),
    ("offs", 0, 0),
    ("w1", 0, 2),
    ("s1", 4, 12),
    ("s2", 0, 12),
    ("w2", 0, 4),
    ("w1", 4, 8),
    ("w1", 8, 12),
    ("w2", 4, 12),
]
PERMS = [(2, 4), (5, 8), (9, 12)]
TAIL = [(0, 512), (512, 256)]


def tile_moe_tk_mlp_silu_kernel(
    tc, xT, w1_words, w1_scales, w2_words, w2_scales, gate, offs, pos1, pos2, pos3, pos4, out
):
    nc = tc.nc
    with ExitStack() as ctx:
        lists = ctx.enter_context(tc.tile_pool(name="lists", bufs=1))
        keep = ctx.enter_context(tc.tile_pool(name="keep", bufs=1))
        ring = ctx.enter_context(tc.tile_pool(name="ring", bufs=4))
        g_ring = ctx.enter_context(tc.tile_pool(name="g_ring", bufs=3))
        a_psum = ctx.enter_context(tc.psum_pool(name="a_psum", bufs=5))
        t_psum = ctx.enter_context(tc.psum_pool(name="t_psum", bufs=1))
        y_psum = ctx.enter_context(tc.psum_pool(name="y_psum", bufs=2))

        warm = keep.tile([P, 1], F32, name="warm")
        warm_out = keep.tile([P, 1], F32, name="warm_out")
        nc.vector.memset(warm[:], 0.0)
        nc.scalar.activation(out=warm_out[:], in_=warm[:], func=SILU)

        raw_s = keep.tile([P, E, H], U8, name="raw_s", align_bytes=64)
        w1_s = keep.tile([P, E, H], U8, name="w1_s", align_bytes=64)
        w2_s = keep.tile([P, E, N], U8, name="w2_s", align_bytes=64)
        for a in range(0, E, 4):
            nc.vector.memset(raw_s[:, a : a + 4, :].bitcast(I32), 0)
        nc.vector.memset(w2_s[:].bitcast(I32), 0)
        x_scales = keep.tile([P, T], U8, name="x_scales", align_bytes=64)
        nc.gpsimd.memset(x_scales[:], 0)
        ident = keep.tile([P, P], F32, name="ident")
        make_identity(nc, ident[:])

        offs_t = lists.tile([P, S // 16], U16, name="offs_t")
        x_view = xT.rearrange("(p j) t -> p j t", j=4)
        x_raw = {}
        raw_w, w2 = {}, {}

        def load(kind, a, b):
            if kind == "offs":
                nc.sync.dma_start(offs_t[:], offs)
            elif kind == "x":
                raw = keep.tile([P, 4, X_CHUNKS[a][1]], F32, name=f"x_raw{a}")
                c = X_CHUNKS[a][0]
                nc.sync.dma_start(raw[:], x_view[:, :, c : c + X_CHUNKS[a][1]])
                x_raw[a] = raw
            elif kind == "s1":
                for q in range(4):
                    rows = w1_scales[a:b, 0, 4 * q : 4 * q + 4, :].rearrange("e q i -> q e i")
                    nc.sync.dma_start(raw_s[32 * q : 32 * q + 4, a:b, :].bitcast(I32), rows.bitcast(I32))
            elif kind == "s2":
                for q in range(4):
                    rows = w2_scales[a:b, 0, 4 * q : 4 * q + 4, :].rearrange("e q n -> q e n")
                    nc.sync.dma_start(w2_s[32 * q : 32 * q + 4, a:b, :].bitcast(I32), rows.bitcast(I32))
            elif kind == "w1":
                words = keep.tile([P, b - a, 2 * H], U8, name=f"raw_w{a}", align_bytes=64)
                nc.sync.dma_start(words[:], w1_words[a:b, 0].rearrange("e p c -> p e c"))
                for e in range(a, b):
                    raw_w[e] = (words, e - a)
            else:
                words = keep.tile([P, b - a, 2 * N], U8, name=f"w2_{a}", align_bytes=64)
                nc.sync.dma_start(words[:], w2_words[a:b, 0].rearrange("e p c -> p e c"))
                for e in range(a, b):
                    w2[e] = words[:, e - a, :]

        for kind, a, b in LOADS:
            load(kind, a, b)
        pos_t = []
        for r, pos in enumerate((pos1, pos2, pos3, pos4)):
            lst = lists.tile([P, T // 16], U16, name=f"pos_t{r}")
            nc.sync.dma_start(lst[:], pos)
            pos_t.append(lst)
        gates = []
        for r in range(TOP):
            g_t = keep.tile([P, T], F32, name=f"gate_t{r}")
            nc.sync.dma_start(g_t[:], gate[r])
            gates.append(g_t)

        w1 = {}

        def permute(a, b):
            words, at = raw_w[a]
            n = b - a
            turned = keep.tile([P, n, 2 * H], U8, name=f"w1_{a}", align_bytes=64)
            nc.vector.tensor_copy(
                out=turned[:].bitcast(U16).rearrange("p e (t m) -> p t e m", t=4),
                in_=words[:, at : at + n, :].bitcast(U16).rearrange("p e (m t) -> p t e m", t=4),
            )
            nc.vector.tensor_copy(
                out=w1_s[:, a:b, :].rearrange("p e (t m) -> p t e m", t=4),
                in_=raw_s[:, a:b, :].rearrange("p e (m t) -> p t e m", t=4),
            )
            for e in range(a, b):
                w1[e] = turned[:, e - a, :]

        x_words = keep.tile([P, T], U32, name="x_words", align_bytes=64)
        x_bf = []
        for i, (a, n) in enumerate(X_CHUNKS):
            xb = keep.tile([P, n, 4], BF16, name=f"x_bf{i}", align_bytes=64)
            x_bf.append(xb)

        def cast(i):
            src = x_raw[i][:].rearrange("p j t -> p t j")
            if i in X_CAST_ON_SCALAR:
                nc.scalar.copy(out=x_bf[i][:], in_=src)
            else:
                nc.vector.tensor_copy(out=x_bf[i][:], in_=src)

        def quantise_x(i):
            a, n = X_CHUNKS[i]
            nc.vector.quantize_mx(
                out=x_words[:, a : a + n].bitcast(FP8X4),
                scales=x_scales[:, a : a + n],
                in_=x_bf[i][:].rearrange("p t j -> p (t j)"),
            )

        cast(0)
        cast(1)
        quantise_x(0)
        quantise_x(1)
        cast(2)
        cast(3)
        quantise_x(2)
        quantise_x(3)

        g_words, g_scales = {}, {}

        def gather(i):
            a, n = GATHERS[i]
            words = g_ring.tile([P, n], U32, name=f"g_words_{n}", align_bytes=64)
            nc.vector.tensor_copy(words[:], x_words[:].indirect(offs_t[:, a // 16 : (a + n) // 16]))
            scales = g_ring.tile([P, n], U8, name=f"g_scales_{n}", align_bytes=64)
            nc.vector.tensor_copy(scales[:], x_scales[:].indirect(offs_t[:, a // 16 : (a + n) // 16]))
            for s in range(0, n, P):
                g_words[(a + s) // P] = words[:, s : s + P]
                g_scales[(a + s) // P] = scales[:, s : s + P]

        y_all = keep.tile([P, S], F32, name="y_all")
        h_bf, h_in, h_words, h_scales, y_ps = {}, {}, {}, {}, {}

        def first(unit):
            g0, count = UNITS[unit]
            e = g0 // 2
            if e in TURNED:
                words, at = raw_w[e]
                for g in range(g0, g0 + count):
                    acc = a_psum.tile([P, H], F32, name="acc")
                    nc.tensor.matmul_mx(
                        out=acc[:],
                        lhsT=g_words[g].bitcast(FP8X4),
                        lhsT_scale=g_scales[g],
                        rhs=words[:, at, :].bitcast(FP4X4),
                        rhs_scale=raw_s[:, e, :],
                        start=True,
                        stop=True,
                    )
                    h = ring.tile([P, H], BF16, name="h", align_bytes=64)
                    nc.scalar.activation(
                        out=h[:].rearrange("s (u p e) -> s u p e", u=2, e=2),
                        in_=acc[:].rearrange("s (p u e) -> s u p e", u=2, e=2),
                        func=SILU,
                    )
                    h_bf[g] = h
                return
            hin = ring.tile([P, count * P, 4], BF16, name=f"hin{count}", align_bytes=64)
            for g in range(count):
                acc = a_psum.tile([P, 4, P], F32, name="acc")
                for t in range(4):
                    nc.tensor.matmul_mx(
                        out=acc[:, t, :],
                        lhsT=w1[e][:, 2 * P * t : 2 * P * (t + 1)].bitcast(FP4X4),
                        lhsT_scale=w1_s[:, e, P * t : P * (t + 1)],
                        rhs=g_words[g0 + g].bitcast(FP8X4),
                        rhs_scale=g_scales[g0 + g],
                        start=True,
                        stop=True,
                    )
                nc.scalar.activation(
                    out=hin[:, g * P : (g + 1) * P, :],
                    in_=acc[:].rearrange("p t s -> p s t"),
                    func=SILU,
                )
            h_in[unit] = hin

        def turn(unit):
            g0, count = UNITS[unit]
            bank = t_psum.tile([P, 2, 2, P], F32, name="bank")
            for g in range(count):
                words = h_bf[g0 + g][:].bitcast(F32)
                for u in range(2):
                    nc.tensor.transpose(bank[:, g, u, :], words[:, u * P : (u + 1) * P], ident[:])
            hin = ring.tile([P, count * P, 4], BF16, name=f"hin{count}", align_bytes=64)
            nc.scalar.copy(
                out=hin[:].bitcast(F32).rearrange("p (g r) u -> p g r u", g=count),
                in_=bank[:, 0:count].rearrange("p g u r -> p g r u"),
            )
            h_in[unit] = hin

        def quantise(unit):
            n = UNITS[unit][1] * P
            hw = ring.tile([P, n], U32, name=f"hw{n}", align_bytes=64)
            hs = ring.tile([P, n], U8, name=f"hs{n}", align_bytes=64)
            nc.vector.quantize_mx(
                out=hw[:].bitcast(FP8X4), scales=hs[:], in_=h_in[unit][:].rearrange("p s j -> p (s j)")
            )
            h_words[unit], h_scales[unit] = hw, hs

        def second(unit):
            g0, count = UNITS[unit]
            e = g0 // 2
            bank = [b for b in Y_BANKS if unit in b][0]
            if unit == bank[0]:
                y_ps[bank] = y_psum.tile([P, 512], F32, name="yp")
            at = (g0 - UNITS[bank[0]][0]) * P
            nc.tensor.matmul_mx(
                out=y_ps[bank][:, at : at + count * P],
                lhsT=w2[e].bitcast(FP4X4),
                lhsT_scale=w2_s[:, e, :],
                rhs=h_words[unit][:].bitcast(FP8X4),
                rhs_scale=h_scales[unit][:],
                start=True,
                stop=True,
            )

        def keep_y(unit):
            bank = [b for b in Y_BANKS if unit in b][0]
            if unit == bank[-1]:
                a = UNITS[bank[0]][0] * P
                n = sum([UNITS[u][1] for u in bank]) * P
                if unit in Y_ON_VECTOR:
                    nc.vector.tensor_copy(out=y_all[:, a : a + n], in_=y_ps[bank][:, 0:n])
                else:
                    nc.scalar.copy(out=y_all[:, a : a + n], in_=y_ps[bank][:, 0:n])

        done = 0
        permuted = 0
        steps = len(UNITS)
        for step in range(steps + 3):
            ahead = UNITS[min(step + 1, steps - 1)][0] * P
            while done < len(GATHERS) and GATHERS[done][0] <= ahead:
                gather(done)
                done += 1
            while permuted < len(PERMS) and PERMS[permuted][0] <= step + 2:
                permute(*PERMS[permuted])
                permuted += 1
            if step < steps:
                first(step)
            if 1 <= step <= steps and UNITS[step - 1][0] // 2 in TURNED:
                turn(step - 1)
            if 2 <= step <= steps + 1:
                quantise(step - 2)
                second(step - 2)
            if 3 <= step:
                keep_y(step - 3)

        prod = []
        part = keep.tile([P, T], F32, name="part")
        total = keep.tile([P, T], F32, name="total")
        res = keep.tile([P, T], F32, name="res")

        def weigh(r):
            term = keep.tile([P, T], F32, name=f"term{r}")
            nc.vector.tensor_tensor(term[:], y_all[:].indirect(pos_t[r][:]), gates[r][:], MULT)
            prod.append(term)

        weigh(0)
        weigh(1)
        weigh(2)
        nc.vector.tensor_tensor(part[:], prod[0][:], prod[1][:], ADD)
        weigh(3)
        for a, n in TAIL:
            cols = slice(a, a + n)
            nc.vector.tensor_tensor(total[:, cols], part[:, cols], prod[2][:, cols], ADD)
        for a, n in TAIL:
            cols = slice(a, a + n)
            nc.vector.tensor_tensor(res[:, cols], total[:, cols], prod[3][:, cols], ADD)
            nc.sync.dma_start(out[:, cols], res[:, cols])
